import numpy as np
import ml_dtypes


def mxq(x, axis, fmt="e4m3"):
    dtype, down = {"e4m3": (ml_dtypes.float8_e4m3fn, 7), "e5m2": (ml_dtypes.float8_e5m2, 14)}[fmt]
    v = np.moveaxis(np.asarray(x, np.float32).astype(ml_dtypes.bfloat16).astype(np.float64), axis, -1)
    blocks = v.reshape(v.shape[:-1] + (-1, 32))
    amax = np.abs(blocks).max(-1, keepdims=True)
    byte = np.maximum(np.where(amax > 0, np.frexp(amax)[1] - 1 + 127, 0) - down, 1)
    scale = np.exp2(byte - 127.0)
    codes = (blocks / scale).astype(np.float32).astype(dtype).astype(np.float64)
    return np.moveaxis((codes * scale).reshape(v.shape), -1, axis)


WIDE = False


def mx_kscale(k):
    if not WIDE:
        return np.ones(k)
    levels = np.array([10, -10, 5, -5, 0])
    if k % 512:
        return np.exp2(np.random.permutation(np.resize(levels, k // 32))).repeat(32)
    a = np.empty((k // 512, 16))
    for p in range(k // 512):
        a[p, :8] = np.random.permutation(np.resize(levels, 8))
        for g in range(8):
            far = levels[np.abs(levels - a[p, g]) >= 10]
            a[p, g + 8] = far[np.random.randint(len(far))]
    return np.exp2(a.ravel()).repeat(32)


BF16 = ml_dtypes.bfloat16


def bf(x):
    return np.asarray(x, np.float32).astype(BF16)


def f64(x):
    return np.asarray(x).astype(np.float64)

E4M3FN = np.array([(-1.0 if i & 128 else 1.0) * ((1.0 + (i & 7) / 8.0) * 2.0 ** (((i >> 3) & 15) - 7) if i & 120 else (i & 7) * 2.0 ** -9) for i in range(256)])


def e4m3fn_bytes(y):
    return np.clip(np.asarray(y, np.float64), -448.0, 448.0).astype(np.float32).astype(ml_dtypes.float8_e4m3fn).view(np.uint8)


def e4m3fn_values(b):
    return E4M3FN[b]


T, N, G = 1024, 2048, 128

E4M3_MAX = 448.0


def setup_inputs():
    s = mx_kscale(N)
    x = np.random.standard_normal((T, N)) / s
    r = np.random.standard_normal((N, N)) / np.sqrt(N) * s
    np.fill_diagonal(r, 0.0)
    x_scale = (np.abs(x).reshape(T, N // G, G).max(axis=2) / E4M3_MAX).astype(np.float32)
    r_scale = (np.abs(r).reshape(N // G, G, N // G, G).max(axis=(1, 3)) / E4M3_MAX).astype(np.float32)
    x_blocks = np.repeat(f64(x_scale), G, axis=1)
    r_blocks = np.repeat(np.repeat(f64(r_scale), G, axis=0), G, axis=1)
    return {"x_bytes": e4m3fn_bytes(x / x_blocks),
            "x_scale": x_scale,
            "r_bytes": e4m3fn_bytes(r / r_blocks),
            "r_scale": r_scale,
            "b": bf(np.random.standard_normal((T, N))),
            "d": bf(np.random.uniform(1.5, 2.5, N))}


def reference(x_bytes, x_scale, r_bytes, r_scale, b, d):
    x = e4m3fn_values(x_bytes) * np.repeat(f64(x_scale), G, axis=1)
    r = e4m3fn_values(r_bytes) * np.repeat(np.repeat(f64(r_scale), G, axis=0), G, axis=1)
    rx = mxq(x, 1, "e4m3") @ mxq(r, 1, "e4m3").T
    return (f64(b) - rx) / f64(d)

from contextlib import ExitStack

import concourse.mybir as mybir
from concourse.masks import make_identity

T, N = 1024, 2048
P = 128
FLOPS = 2 * T * N * N + 2 * T * N

F32 = mybir.dt.float32
BF16 = mybir.dt.bfloat16
U32 = mybir.dt.uint32
U8 = mybir.dt.uint8
FP8 = mybir.dt.float8_e4m3fn
FP8X4 = mybir.dt.float8_e4m3fn_x4
MULT = mybir.AluOpType.mult
SUB = mybir.AluOpType.subtract
COPY = mybir.ActivationFunctionType.Copy

MT = T // P
NG = 4
G = 4
COLS = N // NG

MANUAL = False
LOADS = ['x0', 'r0', 'r1', 'r2', 'r3', 'x1', 'r4', 'r5', 'r6', 'r7', 'x2', 'x3', 'b0', 'r8', 'r9', 'r10', 'r11', 'x4', 'b1', 'x5', 'r12', 'r13', 'r14', 'r15', 'b2', 'x6', 'x7', 'b3']
SEQ = ['x0', 'r0', 'x1', 'r1', 'x2', 'x3', 'r2', 'x4', 'x5', 'r3', 'x6', 'x7']
X_ON_S = (4, 7)
R_ON_V = ()
EX_ON_V = ()
R_EMPTY_ON_S = ((), (2, 3), (2, 3), (2, 3))
DIV_ON_G = (1, 3, 5, 7, 9, 11, 13, 15, 17, 19, 21, 23, 25, 27, 29)
XW_BUFS, RW_BUFS, TMP_BUFS, RES_BUFS = 3, 6, 4, 4
TP_BUFS, ACC_BUFS = 5, 3
DINV_ENGINE, DINV_STEP = 'v', 5
ORDER = 'DSBMWQTE'
WIDEN_AHEAD, LAG, TAIL_QUOTA = 3, 3, 2
STEP_SIZES = (1,) * 24
QUOTAS = (1, 1, 1, 2, 1, 2, 1, 2, 1, 1, 0, 2, 2, 2, 2, 1, 1, 2, 2, 1, 2, 1, 2, 1)


def tile_batched_jacobi_sweep_d2_kernel(tc, x_bytes, x_scale, r_bytes, r_scale, b, d, out):
    nc = tc.nc
    with ExitStack() as ctx:
        keep = ctx.enter_context(tc.tile_pool(name="keep", bufs=1))
        stage = ctx.enter_context(tc.tile_pool(name="stage", bufs=3))
        psum = ctx.enter_context(tc.psum_pool(name="psum", bufs=1))
        if MANUAL:
            ctx.enter_context(tc.manual_schedule())

        d_sb = keep.tile([P, N // P], BF16, name="d_sb")
        xs = keep.tile([P, MT, N // P], F32, name="xs")
        rsb = keep.tile([P, 256], F32, name="rsb")
        rs = keep.tile([P, 64], F32, name="rs")
        dinv = keep.tile([P, N], F32, name="dinv")
        dcol = keep.tile([P, N // P], F32, name="dcol")
        ident = keep.tile([P, P], F32, name="ident")

        xb = [keep.tile([P, N], U8, name="xbytes%d" % m) for m in range(MT)]
        rb = [keep.tile([P, N], U8, name="rbytes%d" % a) for a in range(N // P)]
        bt = [keep.tile([P, MT, COLS], BF16, name="b%d" % n) for n in range(NG)]

        nc.scalar.dma_start(out=xs[:], in_=x_scale.rearrange("(m p) c -> p m c", p=P))
        nc.scalar.dma_start(out=rsb[:], in_=r_scale.rearrange("a c -> (a c)").partition_broadcast(P))
        nc.scalar.dma_start(out=d_sb[:], in_=d.rearrange("(k m) -> k m", m=N // P))
        for tok in LOADS:
            kind, i = tok[0], int(tok[1:])
            if kind == "x":
                nc.sync.dma_start(out=xb[i][:], in_=x_bytes[i * P:(i + 1) * P, :])
            elif kind == "r":
                nc.sync.dma_start(out=rb[i][:], in_=r_bytes[i * P:(i + 1) * P, :])
            else:
                nc.sync.dma_start(out=bt[i][:], in_=b.rearrange("(m p) i -> p m i", p=P)[:, :, i * COLS:(i + 1) * COLS])

        ones = keep.tile([P, 1], F32, name="ones")
        nc.vector.memset(ones[:], 1.0)
        make_identity(nc, ident[:])
        for q in range(4):
            nc.gpsimd.tensor_copy(out=rs[32 * q:32 * q + 32, :], in_=rsb[32 * q:32 * q + 32, q:256:4])
        nc.vector.reciprocal(out=dcol[:], in_=d_sb[:])

        xw = {}
        rw = {}
        xi = {}
        ri = {}
        xc = {}
        rc = {}
        tpx = {}
        acc = {}
        tmp = {}

        def spread_dinv():
            for j in range(4):
                bank = psum.tile([P, 512], F32, tag="acc", bufs=ACC_BUFS, name="dbank%d" % j)
                for i in range(4):
                    nc.tensor.transpose(bank[:, i * P:(i + 1) * P], dcol[:, 4 * j + i:4 * j + i + 1].to_broadcast([P, P]), ident[:])
                dst = dinv[:].rearrange("p (k m) -> p k m", m=16)[:, :, 4 * j:4 * j + 4]
                src = bank[:].rearrange("p (m k) -> p k m", m=4)
                if DINV_ENGINE == "s":
                    nc.scalar.copy(out=dst, in_=src)
                else:
                    nc.vector.tensor_copy(out=dst, in_=src)

        def widen_x(m):
            t = stage.tile([P, N], BF16, tag="xw", bufs=XW_BUFS, name="xw%d" % m)
            xw[m] = t
            src = xb[m][:].bitcast(FP8)
            for c in range(16):
                g, q = c // 4, c % 4
                if m in X_ON_S:
                    nc.scalar.activation(out=t[:, c * P:(c + 1) * P], in_=src[:, c * P:(c + 1) * P], func=COPY, scale=xs[:, m, c:c + 1])
                else:
                    dst = t[:].rearrange("p (g u w e) -> p g u w e", g=4, u=2, e=2)[:, g, :, 32 * q:32 * q + 32, :].rearrange("p u w e -> p w u e")
                    nc.vector.tensor_scalar(out=dst, in0=src[:, c * P:(c + 1) * P], scalar1=xs[:, m, c:c + 1], scalar2=None, op0=MULT)

        def widen_r(a):
            t = stage.tile([P, N], BF16, tag="rw", bufs=RW_BUFS, name="rw%d" % a)
            rw[a] = t
            src = rb[a][:].bitcast(FP8)
            if a in R_ON_V:
                for g in range(4):
                    dst = t[:].rearrange("p (g u w e) -> p g u w e", g=4, u=2, e=2)[:, g, :, :, :].rearrange("p u w e -> p w u e")
                    nc.vector.tensor_scalar(out=dst, in0=src[:, g * 512:(g + 1) * 512], scalar1=ones[:, 0:1], scalar2=None, op0=MULT)
            else:
                nc.scalar.copy(out=t[:], in_=src)

        def turn(bank, slot, words, g, u, packed):
            if packed:
                src = words[:, 256 * g + 128 * u:256 * g + 128 * (u + 1)]
            else:
                src = words[:, 256 * g + u:256 * (g + 1):2]
            nc.tensor.transpose(bank[:, slot * P:(slot + 1) * P], src, ident[:])

        def transpose_x(m):
            words = xw[m][:].bitcast(F32)
            for h in range(2):
                bank = psum.tile([P, 512], F32, tag="tp", bufs=TP_BUFS, name="tpx%d_%d" % (m, h))
                tpx[("x", m, h)] = bank
                for gg in range(2):
                    for u in range(2):
                        turn(bank, 2 * gg + u, words, 2 * h + gg, u, m not in X_ON_S)

        def empty_x(m):
            t = stage.tile([P, N], BF16, tag="xi", bufs=3, align_bytes=64, name="xi%d" % m)
            xi[m] = t
            for h in range(2):
                bank = tpx[("x", m, h)]
                dst = t[:, h * 1024:(h + 1) * 1024].bitcast(F32).rearrange("p (g r u) -> p g r u", g=2, u=2)
                src = bank[:].rearrange("p (g u r) -> p g r u", g=2, u=2)
                if (m, h) in EX_ON_V:
                    nc.vector.tensor_copy(out=dst, in_=src)
                else:
                    nc.scalar.copy(out=dst, in_=src)

        def quant_x(m):
            codes = keep.tile([P, 4 * P], U32, align_bytes=64, name="xcodes%d" % m)
            scales = keep.tile([P, 4 * P], U8, align_bytes=64, name="xplane%d" % m)
            xc[m] = (codes, scales)
            nc.vector.quantize_mx(out=codes[:].bitcast(FP8X4), scales=scales[:], in_=xi[m][:])

        def transpose_r(n, g):
            for h in range(2):
                bank = psum.tile([P, 512], F32, tag="tp", bufs=TP_BUFS, name="tpr%d_%d_%d" % (n, g, h))
                tpx[("r", n, g, h)] = bank
                for aa in range(2):
                    a = 4 * n + 2 * h + aa
                    words = rw[a][:].bitcast(F32)
                    for u in range(2):
                        turn(bank, 2 * aa + u, words, g, u, a in R_ON_V)

        def empty_r(n, g):
            t = stage.tile([P, N], BF16, tag="ri", bufs=3, align_bytes=64, name="ri%d_%d" % (n, g))
            ri[(n, g)] = t
            for al in range(4):
                bank = tpx[("r", n, g, al // 2)]
                dst = t[:, al * 512:(al + 1) * 512].rearrange("p (r u e) -> p r u e", u=2, e=2)
                src = bank[:].bitcast(BF16)[:, (al % 2) * 512:(al % 2 + 1) * 512].rearrange("p (u r e) -> p r u e", u=2, e=2)
                j = (4 * n + al) * 4 + g
                if al in R_EMPTY_ON_S[n]:
                    nc.scalar.activation(out=dst, in_=src, func=COPY, scale=rs[:, j:j + 1])
                else:
                    nc.vector.tensor_scalar(out=dst, in0=src, scalar1=rs[:, j:j + 1], scalar2=None, op0=MULT)

        def quant_r(n, g):
            codes = keep.tile([P, COLS], U32, align_bytes=64, name="rcodes%d_%d" % (n, g))
            scales = keep.tile([P, COLS], U8, align_bytes=64, name="rplane%d_%d" % (n, g))
            rc[(n, g)] = (codes, scales)
            nc.vector.quantize_mx(out=codes[:].bitcast(FP8X4), scales=scales[:], in_=ri[(n, g)][:])

        def product(n, m):
            bank = psum.tile([P, COLS], F32, tag="acc", bufs=ACC_BUFS, name="acc%d_%d" % (n, m))
            acc[(n, m)] = bank
            for g in range(G):
                nc.tensor.matmul_mx(
                    out=bank[:],
                    lhsT=xc[m][0][:, g * P:(g + 1) * P].bitcast(FP8X4),
                    lhsT_scale=xc[m][1][:, g * P:(g + 1) * P],
                    rhs=rc[(n, g)][0][:].bitcast(FP8X4),
                    rhs_scale=rc[(n, g)][1][:],
                    start=(g == 0),
                    stop=(g == G - 1),
                )

        def subtract(n, m):
            t = stage.tile([P, COLS], F32, tag="tmp", bufs=TMP_BUFS, name="tmp%d_%d" % (n, m))
            tmp[(n, m)] = t
            nc.vector.tensor_tensor(out=t[:], in0=bt[n][:, m, :], in1=acc[(n, m)][:], op=SUB)

        def divide(n, m, count):
            t = stage.tile([P, COLS], F32, tag="res", bufs=RES_BUFS, name="res%d_%d" % (n, m))
            eng = nc.gpsimd if count in DIV_ON_G else nc.vector
            eng.tensor_tensor(out=t[:], in0=tmp[(n, m)][:], in1=dinv[:, n * COLS:(n + 1) * COLS], op=MULT)
            nc.sync.dma_start(out=out[m * P:(m + 1) * P, n * COLS:(n + 1) * COLS], in_=t[:])

        flat = []
        for tok in SEQ:
            kind, i = tok[0], int(tok[1:])
            if kind == "x":
                flat.append(("x", i))
            else:
                flat.extend(("r", i, g) for g in range(4))
        steps = []
        i = 0
        for z in STEP_SIZES:
            steps.append(flat[i:i + z])
            i += z
        widen_list = []
        need_count = []
        for st in steps:
            for u in st:
                if u[0] == "x":
                    widen_list.append(("x", u[1]))
                elif u[2] == 0:
                    widen_list.extend(("r", 4 * u[1] + al) for al in range(4))
            need_count.append(len(widen_list))
        widened = 0
        pos = {u: k for k, st in enumerate(steps) for u in st}
        jobs = []
        for n in range(NG):
            for m in range(MT):
                ready = max(pos[("r", n, 3)], pos[("x", m)])
                jobs.append((ready, n, m))
        jobs.sort()
        done = 0
        last = []
        before = []
        divided = 0
        total_steps = len(steps)
        k = 0
        while k < total_steps or done < len(jobs) or last or before:
            now = []
            quota = QUOTAS[k] if k < total_steps else TAIL_QUOTA
            while len(now) < quota and done < len(jobs) and jobs[done][0] + LAG <= k:
                now.append(jobs[done][1:])
                done += 1
            for ch in ORDER:
                if ch == "W" and k < total_steps:
                    target = need_count[min(k + WIDEN_AHEAD, total_steps - 1)]
                    while widened < target:
                        w = widen_list[widened]
                        if w[0] == "x":
                            widen_x(w[1])
                        else:
                            widen_r(w[1])
                        widened += 1
                elif ch == "T" and k < total_steps:
                    for u in steps[k]:
                        if u[0] == "x":
                            transpose_x(u[1])
                        else:
                            transpose_r(u[1], u[2])
                elif ch == "E" and k < total_steps:
                    for u in steps[k]:
                        if u[0] == "x":
                            empty_x(u[1])
                        else:
                            empty_r(u[1], u[2])
                elif ch == "Q" and 1 <= k <= total_steps:
                    for u in steps[k - 1]:
                        if u[0] == "x":
                            quant_x(u[1])
                        else:
                            quant_r(u[1], u[2])
                elif ch == "M":
                    for n, m in now:
                        product(n, m)
                elif ch == "S":
                    for n, m in last:
                        subtract(n, m)
                elif ch == "D":
                    for n, m in before:
                        divide(n, m, divided)
                        divided += 1
                elif ch == "B" and k == DINV_STEP:
                    spread_dinv()
            before = last
            last = now
            k += 1
